import numpy as np, ml_dtypes
CORES = [6,15,38,47]
N = 4
BF = ml_dtypes.bfloat16
L, S, NR, NC, RO, ST = 256, 16, 4096, 1024, 4, 1
def kill(rng, R, share):
    return np.where(rng.random((N, 8, 1, NR)) < share, 64, R)
def shares(rng):
    return np.stack([rng.permutation(np.array([0.1, 0.3, 0.3, 0.5, 0.5, 0.7, 0.7, 0.85])) for q in range(N)])[:, :, None, None]
def parts(rng):
    a = rng.choice(np.array([0.3, 1.0]), (N, 8, 1, NR))
    R = np.clip((16 + 32 * a * (rng.random((N, 8, 16, NR)) - 0.5)).astype(np.int64), 0, 31)
    H = rng.integers(90, 180, (N, 8, RO)) - 12 * np.arange(RO)
    return (rng.integers(0, 256, (N, 8, 16)), kill(rng, R, shares(rng)), rng.integers(0, NR, (N, 8, 16, NC)), rng.integers(0, 4096, (N, 8, NR)),
            rng.integers(0, 32, (N, 8, 16, L)), rng.integers(0, 4096, (N, 8, L)), np.maximum(H, 0))
def pack(w, R, C, P, Z, F, H):
    i = lambda a, *s: np.ascontiguousarray(a.reshape(*s)).astype(np.int32)
    return {"rec": np.ascontiguousarray(R.reshape(N, 128, NR)).astype(np.float32).astype(BF), "cel": i(C, N, 128, NC), "po": i(P, N, 8, NR),
            "pat": np.ascontiguousarray(Z.reshape(N, 128, L)).astype(np.float32).astype(BF), "phi": i(F, N, 8, L), "th": i(H, N, 8, RO), "wt": i(w, N, 128, 1)}
def lowest(ok, c):
    first = np.full((8, NC), L); lane = np.arange(L)[None, :]; g = np.arange(8)[:, None]
    np.minimum.at(first, (np.broadcast_to(g, c.shape), c), np.where(ok, lane, L))
    return ok & (first[g, c] == lane)
def look(R, C, Z, c):
    s = np.take_along_axis(C, c[:, None, :], 2)
    v = np.take_along_axis(R, s.reshape(8, 1, 16 * L), 2).reshape(8, 16, 16, L)
    return s, np.sum(np.abs(v - Z[:, :, None, :]), axis=1), v[:, 0] < 64
def at(a, k):
    return np.take_along_axis(a, k[:, None, :], 1)[:, 0]
def visit(R, C, P, Z, F, w, h, t):
    h1 = h[:, None, None]
    u = np.sum(w[:, :, None] * Z, axis=1) & 4095
    c = ((F * u >> 5) + F + 77 * t) & (NC - 1); e = ((c * u >> 5) + c + 1) & (NC - 1)
    s, d, live = look(R, C, Z, c); s2, d2, live2 = look(R, C, Z, e)
    sup = live & (d < h1); riv = live & (d >= h1)
    gain = 4 * np.sum(np.where(sup, h1 - d, 0), axis=1); loss = np.sum(np.where(riv, d - h1, 0), axis=1)
    acc = lowest(gain >= loss, c)
    has = np.any(sup, axis=1); y = np.argmin(np.where(sup, d, 9999), axis=1); ny = at(s, y)
    foe = np.any(riv, axis=1); nv = at(s, np.argmax(np.where(riv, d, -1), axis=1))
    zn = np.where(has[:, None, :], (Z + np.take_along_axis(R, ny[:, None, :], 2)) >> 1, Z)
    fn = np.where(acc & has, (np.take_along_axis(P, ny, 1) + 5 * at(d, y) + F) & 4095, (5 * F + u) & 4095)
    n = S * np.arange(L)[None, :] + (u & (S - 1))
    R2 = R.copy(); C2 = C.copy(); P2 = P.copy()
    g, i = np.nonzero(acc & foe); R2[g, :, nv[g, i]] = 64
    g, i = np.nonzero(acc); R2[g, :, n[g, i]] = zn[g, :, i]; P2[g, n[g, i]] = fn[g, i]
    g, i = np.nonzero(acc & np.any(~live, axis=1)); row = np.argmax(~live, axis=1)
    C2[g, row[g, i], c[g, i]] = n[g, i]
    acc2 = lowest(acc & ~np.any(live2 & (d2 < h1), axis=1), e)
    g, i = np.nonzero(acc2 & np.any(~live2, axis=1)); row = 15 - np.argmax(~live2[:, ::-1], axis=1)
    C2[g, row[g, i], e[g, i]] = n[g, i]
    return R2, C2, P2, zn, fn, acc
def setup_inputs(rng):
    return pack(*parts(rng))
def setup_inputs_spread(rng):
    w, R, C, P, Z, F, H = parts(rng)
    R = np.minimum((32 * rng.random((N, 8, 16, NR)) ** np.exp2(rng.integers(-2, 3, (N, 8, 1, NR)))).astype(np.int64), 31)
    Z = np.minimum((32 * rng.random((N, 8, 16, L)) ** np.exp2(rng.integers(-2, 3, (N, 8, 1, L)))).astype(np.int64), 31)
    C = np.minimum((NR * rng.random((N, 8, 16, NC)) ** 3).astype(np.int64), NR - 1)
    P = np.minimum(np.exp2(12 * rng.random((N, 8, NR))).astype(np.int64), 4095); F = np.minimum(np.exp2(12 * rng.random((N, 8, L))).astype(np.int64), 4095)
    w = np.minimum(np.exp2(8 * rng.random((N, 8, 16))).astype(np.int64), 255)
    H = np.where(rng.random((N, 8, RO)) < 0.6, rng.integers(60, 220, (N, 8, RO)), rng.integers(0, 481, (N, 8, RO)))
    return pack(w, kill(rng, R, shares(rng)), C, P, Z, F, H)
def edge(rng, n):
    k = rng.integers(0, 4, (N, 8, 1, n))
    return 31 * np.where(k <= 1, 0, np.where(k == 2, 1, rng.integers(0, 2, (N, 8, 16, n))))
def setup_inputs_ends(rng):
    w = 255 * rng.integers(0, 2, (N, 8, 16)); R = kill(rng, edge(rng, NR), 0.4); Z = edge(rng, L)
    C = np.where(rng.random((N, 8, 16, NC)) < 0.7, (NR - 1) * rng.integers(0, 2, (N, 8, 16, NC)), rng.integers(0, NR, (N, 8, 16, NC)))
    P = 4095 * rng.integers(0, 2, (N, 8, NR)); F = 4095 * rng.integers(0, 2, (N, 8, L)); H = 480 * rng.integers(0, 2, (N, 8, RO))
    for q in range(N):
        for g in range(6):
            R[q, g, :, 0] = (0, 31, 64)[(q + g) % 3]; R[q, g, :, NR - 1] = (0, 31, 64)[(q + g + 1) % 3]
    w[:, 5] = 0; w[:, 5, 0] = 195; Z[:, 5, 0, 0] = 21; F[:, 5, 0] = 4095
    R[:, 6] = 64; Z[:, 6] = 0; F[:, 6] = 0
    H[:, 7, 0] = 0; H[:, 7, 1] = 480; R[:, 7, :, 0] = 31; R[:, 7, :, NR - 1] = 0
    C[:, 7, :, 0] = 0; C[:, 7, :, NC - 1] = 0; C[:, 7, :, 77] = NR - 1
    for k in (0, 5, L - 2, L - 1):
        Z[:, 7, :, k] = 0; F[:, 7, k] = 0
    for q in range(N):
        a = visit(R[q], C[q], P[q], Z[q], F[q], w[q], H[q, :, 0], 0)[5]; a[6] = False
        m = 1 + ((30 - int(np.count_nonzero(a))) & 31)
        F[q, 6, rng.permutation(L)[:m - 1]] = np.arange(1, m)
    return pack(w, R, C, P, Z, F, H)
def selfsame(rng, u0, p0):
    p = np.arange(4096)[:, None]; u = np.arange(256)[None, :]
    c = ((p * u >> 5) + p) & (NC - 1); e = ((c * u >> 5) + c + 1) & (NC - 1)
    c0 = ((p0 * u0 >> 5) + p0) & (NC - 1); e0 = ((c0 * u0 >> 5) + c0 + 1) & (NC - 1)
    i, j = np.nonzero((c == e) & (c != c0) & (c != e0)); z = int(rng.integers(0, len(i)))
    return int(j[z]), int(i[z])
def setup_inputs_corners(rng):
    w, R, C, P, Z, F, H = parts(rng)
    for q in range(N):
        for g in range(8):
            o = (g + q) & 7
            if o == 0:
                R[q, g] = 64; Z[q, g] = 0; F[q, g] = rng.permutation(NC)[:L]
                w[q, g] = 0; w[q, g, 0] = 163; Z[q, g, 0, 0] = 25; F[q, g, 0] = 4093
                u, p = selfsame(rng, 4075, 4093)
                w[q, g, 1] = 1; w[q, g, 2] = 32; Z[q, g, 1, 1] = u & 31; Z[q, g, 2, 1] = u >> 5; F[q, g, 1] = p
            elif o == 1:
                R[q, g] = rng.integers(0, 32, (16, NR))
            elif o == 2:
                h = NR // 2; R[q, g, :, :h] = rng.integers(0, 32, (16, h)); R[q, g, :, h:] = 64
                C[q, g] = rng.integers(0, h, (16, NC)) + h * (np.arange(NC) & 1)[None, :]
                C[q, g, 15, 2::4] = h + rng.integers(0, h, NC // 4); C[q, g, 0, 3::4] = rng.integers(0, h, NC // 4)
            elif o == 3:
                C[q, g] = rng.integers(0, NR, (1, NC))
            elif o == 4:
                w[q, g] = 0; C[q, g] = S * rng.integers(0, L, (16, NC))
            elif o == 5:
                H[q, g] = 0; R[q, g] = np.where(R[q, g, :1] == 64, 64, 7 + (rng.random((1, NR)) < 0.1)); Z[q, g] = 7 + (rng.random((1, L)) < 0.1)
            elif o == 6:
                H[q, g] = 480; R[q, g] = np.where(R[q, g, :1] == 64, 64, 31 * rng.integers(0, 2, (1, NR))); Z[q, g] = 31 * rng.integers(0, 2, (1, L))
            else:
                w[q, g] = 255; C[q, g] = rng.choice(np.array([0, 1, S - 1, S, NR - S, NR - 2, NR - 1]), (16, NC))
                F[q, g] = 4095 * rng.integers(0, 2, L); P[q, g] = 4095 * rng.integers(0, 2, NR)
    return pack(w, R, C, P, Z, F, H)
def meet(rng):
    p = rng.integers(0, 4096, 1024)[:, None]; u = np.arange(1024)[None, :]
    c = ((p * u >> 5) + p) & (NC - 1); e = ((c * u >> 5) + c + 1) & (NC - 1); k = e[int(rng.integers(0, 1024)), int(rng.integers(512, 1024))]
    i, j = np.nonzero(e == k); o = rng.permutation(len(i)); i, j = i[o], j[o]
    x = np.resize(rng.permutation(np.unique(c[i, j], return_index=True)[1]), L); i, j = i[x], j[x]
    a, b = np.nonzero((e != k) & ~np.isin(c, c[i, j])); z = int(rng.integers(0, len(a)))
    return u[0, j], p[i, 0], int(u[0, b[z]]), int(p[a[z], 0])
def setup_inputs_crowd(rng):
    w, R, C, P, Z, F, H = parts(rng)
    for q in range(N):
        for g in range(8):
            o = (g + q) & 7; f0 = int(rng.integers(0, 4095))
            if q < 2:
                R[q, g] = 64; Z[q, g] = 0; F[q, g] = rng.permutation(NC)[:L]; H[q, g, 1] = int(rng.integers(220, 260))
            elif o <= 2:
                Z[q, g] = Z[q, g, :, :1].copy(); F[q, g] = f0; H[q, g, 0] = 480
                if o == 1: F[q, g, L - 1] = f0 + 1
                if o == 2: F[q, g, 1::2] = f0 + 1
            elif o <= 4:
                u, p, u1, p1 = meet(rng)
                if o == 4: u[L - 1] = u1; p[L - 1] = p1
                w[q, g] = 0; w[q, g, 0] = 1; w[q, g, 1] = 32; R[q, g] = 64; Z[q, g, 0] = u & 31; Z[q, g, 1] = u >> 5; F[q, g] = p
            elif o <= 6:
                w[q, g] = 0; R[q, g] = rng.integers(0, 4, (16, NR)); R[q, g, :, NR - 1] = 31; Z[q, g] = rng.integers(0, 4, (16, L)); F[q, g] = rng.permutation(NC)[:L]; H[q, g, 0] = 200
                C[q, g] = rng.integers(0, NR - 1, (16, NC)); C[q, g, rng.integers(0, 16, NC), np.arange(NC)] = NR - 1
                if o == 6: C[q, g, :, F[q, g, 3]] = rng.integers(0, NR - 1, 16)
            else:
                w[q, g] = 0; F[q, g] = f0; H[q, g, 0] = 150
    F[1, 7, L - 1] = F[1, 7, 0]
    return pack(w, R, C, P, Z, F, H)
def setup_inputs_ties(rng):
    w, R, C, P, Z, F, H = parts(rng)
    R = kill(rng, 8 * rng.integers(0, 2, (N, 8, 16, NR)), shares(rng)); Z = 8 * rng.integers(0, 2, (N, 8, 16, L)); H = 8 * rng.integers(4, 11, (N, 8, RO))
    C[:, :, 15] = np.where(rng.random((N, 8, NC)) < 0.3, C[:, :, 0], C[:, :, 15])
    return pack(w, R, C, P, Z, F, H)
def check_inputs(d):
    bad = []
    for k, lo, hi in (("rec", 0, 64), ("cel", 0, NR - 1), ("po", 0, 4095), ("pat", 0, 31), ("phi", 0, 4095), ("th", 0, 480), ("wt", 0, 255)):
        a = np.asarray(d[k]).astype(np.float64)
        if not (np.min(a) >= lo and np.max(a) <= hi and np.all(a == np.floor(a))): bad.append("range of " + k)
    a = np.asarray(d["rec"]).astype(np.float32).reshape(N, 8, 16, NR)
    if not np.all(np.all(a == 64, axis=2) | np.all(a <= 31, axis=2)): bad.append("a record of rec is neither living nor dead")
    return bad
def reference(rec, cel, po, pat, phi, th, wt):
    R = list(rec.astype(np.float32).astype(np.int32).reshape(N, 8, 16, NR)); C = list(cel.astype(np.int32).reshape(N, 8, 16, NC)); P = list(po.astype(np.int64))
    Z = list(pat.astype(np.float32).astype(np.int32).reshape(N, 8, 16, L)); F = list(phi.astype(np.int64))
    w = wt.astype(np.int32).reshape(N, 8, 16); H = th.astype(np.int64); A = [0] * N
    for t in range(RO):
        for q in range(N):
            R[q], C[q], P[q], Z[q], F[q], acc = visit(R[q], C[q], P[q], Z[q], F[q], w[q], H[q, :, t] + (A[q] & 31), t)
            A[q] = int(np.count_nonzero(acc))
        Z = [Z[(q - ST) % N] for q in range(N)]; F = [F[(q - ST) % N] for q in range(N)]
    return {"yrec": np.stack(R).reshape(N, 128, NR).astype(np.float32).astype(BF), "ycel": np.stack(C).reshape(N, 128, NC).astype(np.float32), "ypo": np.stack(P).astype(np.float32),
            "ypat": np.stack(Z).reshape(N, 128, L).astype(np.float32).astype(BF), "yphi": np.stack(F).astype(np.float32)}

from concourse.mybir import AluOpType as A, AxisListType, ActivationFunctionType as F

NV = 4
CH = [(0, 4), (4, 4), (8, 4), (12, 4)]
CM = ["a", "v", "a", "v"]
ZM = ["g", "a"] * 8
EM = ["v", "v", "v", "v", "v", "a", "a", "a"]
TRN = 3.0
CY = 0.83e-3 * 1.2

B, H, F4, I4, U2 = "bfloat16", "float16", "float32", "int32", "uint16"
SHAPES = {
    B: "R:4608 x2:4096 ze:4096 ve:4096 sup:256 sg:256 sg2:256 xs:256 x4:256 zh:256 ckb:256 mM:256 s64:256 accb:16",
    H: "crow:256 vrow:256 winr:256 sa_:256 sb_:256 sq_:256 pg:256 phh:256 thh:4 Bh:128 Ih:128 r16h:256 L3:48 v16:16",
    F4: "C:1280 PT:4352 posf:256 erF:256 sF:256 sF2:256 nd:256 nd2:256 sm:256 kr:256 sx:256 phr:256 thf:4 hc:8 hA:4 hB:4 hm:4 "
        "B8a:8 B8:8 g16:8 g16b:8 K3:48 rc:2 Cr:256 d0n:256 d0x:256 ck:256 par:2 r16:256 RM:48 acc:32 T2c:32 la:32 col:16",
    I4: "Ci:1024 pos:256 phl:256 thl:4 wl:1 ai:1 CI:48",
    U2: "su:256 su2:256 lau:32",
}
LF = "u32 has t3 t4 t5 ps pdh w5 w6 f0 f0a dif ph rr dl l2 foe flg vk unq cnd cn0 w2 vrm nek cf jr I16 b256 i16 zt iL tr tc pw pwb".split()
LI = "ui u2 xq xr ye kI ny w1 fI vs fr fr2".split()
LU = "cu eu zo nyu dlu l2u".split()
MB = "Bb W1 Do Dg Zb Ib In Y1 Y2".split()
MF = "one idf Bba Bf shp shm Utf Ulf".split()
SCRATCH = {}
for _d, _l in SHAPES.items():
    for _x in _l.split():
        SCRATCH[_x.split(":")[0]] = ("sbuf", [128, int(_x.split(":")[1])], _d)
for _x in ("xa", "xe", "EQ", "EQe", "EQv"):
    SCRATCH[_x] = ("sbuf", [128, 16, 256], B)
for _x, _d in (("Sb", B), ("Sk", B), ("Sw", B), ("Sh", H), ("Pk", H), ("Sp", H)):
    SCRATCH[_x] = ("sbuf", [128, 16, 128], _d)
for _x, _l, _n, _d in (("lf", LF, 16, F4), ("li", LI, 16, I4), ("lu", LU, 16, U2), ("mb", MB, 128, B), ("mf", MF, 128, F4)):
    SCRATCH[_x] = ("sbuf", [128, len(_l), _n], _d)
SCRATCH["s16"] = ("sbuf", [128, 8, 2, 16], H)
SCRATCH["t16"] = ("sbuf", [128, 8, 32], H)
SCRATCH["W4"] = ("sbuf", [128, 4, 128], H)
for _t in range(NV + 1):
    SCRATCH["zin%d" % _t] = ("sbuf", [128, 256], B)
    SCRATCH["fin%d" % _t] = ("sbuf", [128, 16], H)
for _t in range(NV):
    SCRATCH["zout%d" % _t] = ("sbuf", [128, 256], B)
    SCRATCH["fout%d" % _t] = ("sbuf", [128, 16], H)
for _b in range(8):
    SCRATCH["b%d" % _b] = ("psum", [128, 512], F4)
DMAS = ["rec", "cel", "wt", "pat", "phi", "th", "po", "pt", "yrec", "ycel", "ypo", "ypat", "yphi"]
SEMAPHORES = ["qv", "qa", "qp", "qg"] + ["d" + n for n in DMAS] + ["%s%d" % (k, t) for k in ("zr", "zl", "fr", "fl") for t in range(NV)]


def dv(n, rate=1.0, k=1):
    return k * max(64, n * rate + 12) * CY


def dp(n, k=1):
    return k * max(64, n) * 0.45e-3 + 0.03


def program(T, g, me, nxt, topo):
    v, a, p, s = g.vector, g.scalar, g.tensor, g.sync
    ops = []
    last = {}

    def add(q, fns, w, r, d, sem=None, val=0, net=None):
        o = {"q": q, "f": fns, "d": d, "sem": sem, "val": val, "i": len(ops), "wait": set(), "ord": set(), "net": net}
        rs, ws = r.split(), w.split()
        for key in sorted(set(rs + ws)):
            L = last.setdefault(key, [None, []])
            if key[0] == "b" and key[1:].isdigit():
                if L[0] is not None:
                    free = ops[L[0]]["q"] == q and (q == "p" or not L[1])
                    o["ord" if free else "wait"].add(L[0])
                last[key] = [o["i"], key in ws]
                continue
            if key in rs and L[0] is not None:
                o["wait"].add(L[0])
            if key in ws:
                for x in ([L[0]] if L[0] is not None else []) + L[1]:
                    o["ord" if ops[x]["q"] == q and ops[x]["sem"] is None and x != L[0] else "wait"].add(x)
                last[key] = [o["i"], []]
            else:
                L[1].append(o["i"])
        o["ord"] -= o["wait"]
        ops.append(o)
        return o["i"]

    def V(fn, w, r, n, rate=1.0):
        return add("v", [fn], w, r, dv(n, rate))

    def S_(fn, w, r, n, rate=1.0):
        return add("a", [fn], w, r, dv(n, rate))

    def G(fn, w, r, n):
        return add("g", [fn], w, r, 0.2 + 2 * n * CY)

    def PM(args, n, w, r):
        return add("p", [(lambda x=x: p.matmul(*x)) for x in args], w, r, dp(n, len(args)))

    def D(name, out, in_, w, r, d, q="s"):
        return add(q, [lambda: (s if q == "s" else a).dma_start(out, in_)], w, r, d, "d" + name, 16)

    TS, TT, TC, MS, ACT = v.tensor_scalar, v.tensor_tensor, v.tensor_copy, v.memset, a.activation
    RED = lambda out, in_: v.tensor_reduce(out, in_, AxisListType.X, A.add)
    R16 = range(16)
    (u32, has, t3, t4, t5, ps, pdh, w5, w6, f0, f0a, dif, ph, rr, dl, l2, foe, flg, vk, unq, cnd, cn0, w2, vrm, nek, cf, jr, I16, b256, i16, zt, iL,
     tr, tc, pw, pwb) = [T.lf[:, k, :] for k in range(len(LF))]
    ui, u2, xq, xr, ye, kI, ny, w1, fI, vs, fr, fr2 = [T.li[:, k, :] for k in range(len(LI))]
    cu, eu, zo, nyu, dlu, l2u = [T.lu[:, k, :] for k in range(len(LU))]
    Bb, W1, Do, Dg, Zb, Ib, In, Y1, Y2 = [T.mb[:, k, :] for k in range(len(MB))]
    one, idf, Bba, Bf, shp, shm, Utf, Ulf = [T.mf[:, k, :] for k in range(len(MF))]
    pc, gs, jc, j16, p2, wf, bn, bx, af = [T.col[:, k:k + 1] for k in range(9)]
    lfc = lambda name, b: T.lf[:, LF.index(name), b:b + 1]

    def pick(out, src, bank):
        PM([(out, T.Pk[:, j, :], T[src][:, j:256:16], j == 0, j == 15) for j in R16], 16, bank, "Pk " + src)

    def spread(bank, off, src, lo, hi):
        PM([(T[bank][:, off + j:off + 16 * (hi - lo):16], T.Sp[:, j, :], T[src][:, lo:hi], True, True) for j in R16], hi - lo, bank, "Sp " + src)

    V(lambda: MS(T.phl[:], 0), "phl", "", 256)
    V(lambda: MS(T.thl[:], 0), "thl", "", 4)
    D("pat", T.zin0[:], T.pat[:], "zin0", "", 2.0)
    D("wt", T.wl[:], T.wt[:], "wl", "", 2.0)
    D("phi", T.phl[0:128:16, :], T.phi[:], "phl", "", 2.0)
    D("cel", T.Ci[:], T.cel[:], "Ci", "", 3.5)
    D("rec", T.R[:, 0:4096], T.rec[:], "R", "", 6.0, "a")
    D("th", T.thl[0:128:16, :], T.th[:], "thl", "", 2.0)
    D("po", T.pos[:], T.po[:], "pos", "", 2.0)
    V(lambda: MS(one, 1.0), "one", "", 128)
    iota = lambda out, pat, base=0, cm=0: g.iota(out, pat, base, cm, allow_small_or_imprecise_dtypes=True)
    sel = lambda out, in_, pat, op, base, cm: g.affine_select(out, in_, pat, op, 0.0, base, cm)
    G(lambda: sel(T.B8a[:], T.mf[:, 0, 0:8], [[-16, 8]], A.is_ge, 0, 1), "B8a", "one", 8)
    G(lambda: sel(T.B8[:], T.B8a[:], [[16, 8]], A.is_ge, 15, -1), "B8", "B8a", 8)
    G(lambda: iota(T.g16[:], [[16, 8]]), "g16", "", 8)
    G(lambda: iota(pc, [[0, 1]], 0, 1), "pc", "", 1)
    G(lambda: iota(jr, [[1, 16]]), "jr", "", 16)
    G(lambda: iota(b256, [[256, 16]]), "b256", "", 16)
    G(lambda: sel(idf, one, [[-1, 128]], A.is_equal, 0, 1), "idf", "one", 128)
    G(lambda: sel(Bba, one, [[-16, 8], [0, 16]], A.is_ge, 0, 1), "Bba", "one", 128)
    G(lambda: sel(Bf, Bba, [[16, 8], [0, 16]], A.is_ge, 15, -1), "Bf", "Bba", 128)
    V(lambda: MS(T.Sb[:], 0.0), "Sb", "", 2048, 0.5)
    add("v", [(lambda j=j: TC(T.Sb[:, j, j:128:16], T.B8[:])) for j in R16], "Sb", "B8", dv(8, 1, 16))
    V(lambda: TC(wf, T.wl[:]), "wf", "wl", 1)
    V(lambda: TS(T.Sw[:], T.Sb[:], wf, None, A.mult), "Sw", "Sb wf", 2048, 0.5)
    V(lambda: TC(T.C[:, 0:1024], T.Ci[:]), "C", "Ci", 1024)
    V(lambda: MS(T.C[:, 1024:1280], 0.0), "C", "", 256)
    S_(lambda: ACT(T.Sk[:], T.Sb[:], F.Copy, scale=65536.0), "Sk", "Sb", 2048)
    V(lambda: TT(T.g16b[:], T.g16[:], T.B8[:], A.mult), "g16b", "g16 B8", 8)
    V(lambda: RED(gs, T.g16b[:]), "gs", "g16b", 8)
    V(lambda: TT(jc, pc, gs, A.subtract), "jc", "pc gs", 1)
    V(lambda: TS(I16, jr, jc, None, A.is_equal), "I16", "jr jc", 16)
    V(lambda: TS(j16, jc, 16.0, None, A.mult), "j16", "jc", 1)
    V(lambda: TS(bn, jc, -1.0, None, A.mult), "bn", "jc", 1)
    V(lambda: TS(bx, jc, -15.0, None, A.add), "bx", "jc", 1)
    V(lambda: TS(i16, b256, j16, None, A.add), "i16", "b256 j16", 16)
    V(lambda: TS(iL, i16, 0.0625, None, A.mult), "iL", "i16", 16)
    V(lambda: TS(tr, iL, 4096.0, None, A.add), "tr", "iL", 16)
    V(lambda: TS(tc, iL, 1024.0, None, A.add), "tc", "iL", 16)
    V(lambda: TS(zt, iL, 4352.0, None, A.add), "zt", "iL", 16)
    V(lambda: TT(T.K3[:, 0:16], tr, i16, A.subtract), "K3", "i16 tr", 16)
    V(lambda: TC(T.K3[:, 16:32], tc), "K3", "tc", 16)
    V(lambda: TC(T.K3[:, 32:48], tc), "K3", "tc", 16)
    V(lambda: TC(T.T2c[:, 0:16], tr), "T2c", "tr", 16)
    V(lambda: TC(T.T2c[:, 16:32], tc), "T2c", "tc", 16)
    for k, (x, y) in enumerate(((65536.0, -16777216.0), (65536.0, 61440.0 - 16777216.0), (1.0, -512.0), (80.0, 0.0))):
        V(lambda k=k, x=x: MS(T.hA[:, k:k + 1], x), "hA", "", 1)
        V(lambda k=k, y=y: MS(T.hB[:, k:k + 1], y), "hB", "", 1)
    V(lambda: TC(T.Sh[:], T.Sb[:]), "Sh", "Sb", 2048, 0.5)
    V(lambda: TS(T.Pk[:], T.Sb[:], lfc("I16", 0), None, A.mult), "Pk", "Sb I16", 2048, 0.5)
    V(lambda: TC(Bb, Bf), "Bb", "Bf", 128)
    V(lambda: TC(T.Bh[:], Bf), "Bh", "Bf", 128)
    add("v", [(lambda j=j: TS(T.Sp[:, j, :], Bb, lfc("I16", j), None, A.mult)) for j in R16], "Sp", "Bb I16", dv(128, 0.5, 16))
    V(lambda: RED(T.rc[:, 0:1], T.B8[:, 0:8:2]), "rc", "B8", 4)
    V(lambda: RED(T.rc[:, 1:2], T.B8[:, 1:8:2]), "rc", "B8", 4)
    G(lambda: sel(shp, one, [[-1, 128]], A.is_equal, 16, 1), "shp", "one", 128)
    G(lambda: sel(shm, one, [[-1, 128]], A.is_equal, -16, 1), "shm", "one", 128)
    for k, (src, key, r) in enumerate(((idf, "idf", 0), (shp, "shp", 0), (shm, "shm", 1), (idf, "idf", 1))):
        V(lambda k=k, src=src, r=r: TS(T.W4[:, k, :], src, T.rc[:, r:r + 1], None, A.mult), "W4", key + " rc", 128)
    G(lambda: iota(T.ck[:], [[0, 16], [4096, 16]], 2048), "ck", "", 256)
    V(lambda: RED(T.par[:, 0:1], T.lf[:, LF.index("I16"), 0:16:2]), "par", "I16", 8)
    V(lambda: TS(T.par[:, 1:2], T.par[:, 0:1], 16777216.0, -16777216.0, A.mult, A.add), "par", "par", 1)
    V(lambda: TS(T.ckb[:], T.ck[:], T.par[:, 0:1], T.par[:, 1:2], A.mult, A.add), "ckb", "ck par", 256)
    V(lambda: MS(W1, 0.015625), "W1", "", 128, 0.5)
    G(lambda: iota(T.r16[:], [[16, 256]]), "r16", "", 256)
    V(lambda: TC(T.r16h[:], T.r16[:]), "r16h", "r16", 256)
    V(lambda: TC(T.Ih[:], idf), "Ih", "idf", 128)
    V(lambda: TC(Ib, idf), "Ib", "idf", 128)
    V(lambda: TS(In, idf, -1.0, None, A.mult), "In", "idf", 128)
    V(lambda: MS(T.d0n[:], 0.0), "d0n", "", 256)
    V(lambda: MS(T.d0n[:, 0:256:16], 134217728.0), "d0n", "", 16)
    add("v", [(lambda j=j: MS(T.Cr[:, j:256:16], float(2 ** (16 - j)))) for j in R16], "Cr", "", dv(16, 1, 16))
    V(lambda: TS(pw, T.Cr[:, 0:16], 0.5, None, A.mult), "pw", "Cr", 16)
    V(lambda: TT(pwb, pw, I16, A.mult), "pwb", "pw I16", 16)
    V(lambda: RED(p2, pwb), "p2", "pwb", 16)
    V(lambda: TS(Do, Bb, 65536.0, None, A.mult), "Do", "Bb", 128, 0.5)
    V(lambda: TS(Dg, Bb, p2, None, A.mult), "Dg", "Bb p2", 128, 0.5)
    V(lambda: MS(Zb, 0.0), "Zb", "", 128, 0.5)
    V(lambda: MS(T.s64[:], 64.0), "s64", "", 256, 0.5)
    V(lambda: MS(T.d0x[:], 8192.0), "d0x", "", 256)
    V(lambda: MS(T.d0x[:, 0:256:16], -268435456.0), "d0x", "", 16)
    G(lambda: sel(Utf, Bf, [[1, 128]], A.is_gt, 0, -1), "Utf", "Bf", 128)
    G(lambda: sel(Ulf, Bf, [[-1, 128]], A.is_gt, 0, 1), "Ulf", "Bf", 128)
    V(lambda: TT(Y1, idf, Utf, A.subtract), "Y1", "idf Utf", 128, 2)
    V(lambda: TT(Y2, idf, Ulf, A.subtract), "Y2", "idf Ulf", 128, 2)
    G(lambda: iota(T.PT[:], [[0, 4352]]), "PT", "", 4352)
    V(lambda: MS(T.R[:, 4096:4352], 0.0), "R", "", 256, 0.5)
    V(lambda: TC(T.thh[:], T.thl[:]), "thh", "thl", 4)
    PM([(T.b3[:, 64:68], T.Bh[:], T.thh[:], True, True)], 4, "b3", "Bh thh")
    V(lambda: TC(T.thf[:], T.b3[:, 64:68]), "thf", "b3", 4)
    V(lambda: TS(T.phh[:], T.phl[:], -2048.0, None, A.add), "phh", "phl", 256)
    pick(T.b5[:, 256:272], "phh", "b5")
    V(lambda: TC(T.fin0[:], T.b5[:, 256:272]), "fin0", "b5", 16)
    V(lambda: TC(T.posf[:], T.pos[:]), "posf", "pos", 256)
    D("pt", T.PT[0:128:16, 0:4096], T.posf[:], "PT", "posf", 2.5)

    def dedupe(eq, bank, eng, row, rkey, key, flag):
        for q in range(4):
            bs = range(4 * q, 4 * q + 4)
            e = lambda b: T[eq][:, b, 0:256 - 16 * b]
            ek = "%s.%d" % (eq, q)
            if eng == "v":
                add("v", [(lambda b=b: TS(e(b), row[:, 16 * b:256], lfc(key, b), lfc(flag, b), A.is_equal, A.mult)) for b in bs],
                    ek, "%s %s %s" % (rkey, key, flag), sum(dv(256 - 16 * b, 0.5) for b in bs))
            else:
                d = sum(dv(256 - 16 * b) for b in bs)
                add("a", [(lambda b=b: ACT(e(b), row[:, 16 * b:256], F.Square, bias=lfc(key, b))) for b in bs], ek, rkey + " " + key, d)
                add("a", [(lambda b=b: ACT(e(b), e(b), F.Relu, bias=lfc(flag, b), scale=-1.0)) for b in bs], ek, ek + " " + flag, d)
        for q in range(4):
            bs = range(4 * q, 4 * q + 4)
            ms = [] if q else [(T[bank][:, 0:256], Zb, T.s64[:], True, False)]
            ms += [(T[bank][:, 16 * b + 16:256], Do, T[eq][:, b, 16:256 - 16 * b], False, False) for b in bs if b < 15]
            if q == 3:
                ms.append((T[bank][:, 0:256], Dg, T[eq][:, :, 0:16], False, True))
            PM(ms, 200 - 40 * q, bank, ("%s.%d Do" % (eq, q)) + (" Zb s64" if not q else "") + (" Dg @.0 @.1 @.2".replace("@", eq) if q == 3 else ""))
        V(lambda: TT(T.winr[:], T[bank][:, 0:256], T.Cr[:], A.is_lt), "winr", bank + " Cr", 256)
        pick(T[bank][:, 256:272], "winr", bank)

    def send(key, src, dst, t):
        rid, pid, _ = topo.addr(nxt)
        m, n = topo.mask(me, nxt), len(topo.engines(me, nxt))
        i = add("g", [lambda: g.remote_dma(T[dst][:], T[src][:], T.sem["%sr%d" % (key, t)], T.sem["%sl%d" % (key, t)], pid, rid, m)],
                "", src, 0.3, "%sl%d" % (key, t), n)
        add("n", [], dst, "", TRN, "%sr%d" % (key, t), n, i)

    ZE = " ".join("ze.%d" % k for k in R16)
    WB = T.b5[:, 256:272]
    for t in range(NV):
        zi, fi, zo_, fo = "zin%d" % t, "fin%d" % t, "zout%d" % t, "fout%d" % t
        zin, fin, zout, fout = T[zi], T[fi], T[zo_], T[fo]
        PM([(T.b3[:, 0:16], T.Sw[:, j, :], zin[:, j:256:16], j == 0, j == 15) for j in R16], 16, "b3", "Sw " + zi)
        V(lambda: TC(xr, T.b3[:, 0:16]), "xr", "b3", 16)
        V(lambda: TS(ui, xr, 4095, None, A.bitwise_and), "ui", "xr", 16)
        V(lambda: TS(u32, ui, 32.0, None, A.add), "u32", "ui", 16)
        V(lambda t=t: TS(u2, ui, 2048.0, 2464.0 * t, A.mult, A.add), "u2", "ui", 16)
        V(lambda: TS(u2, u2, 32767, None, A.bitwise_and), "u2", "u2", 16)
        for k in R16:
            zk = T.ze[:, k:4096:16]
            if ZM[k] == "a":
                S_(lambda zk=zk, zin=zin: ACT(zk, zin[:], F.Copy), "ze.%d" % k, zi, 256)
            elif ZM[k] == "g":
                G(lambda zk=zk, zin=zin: sel(zk, zin[:], [[0, 256]], A.is_gt, 1, 0), "ze.%d" % k, zi, 256)
            else:
                V(lambda zk=zk, zin=zin: TC(zk, zin[:]), "ze.%d" % k, zi, 256, 0.5)
        S_(lambda zin=zin: ACT(T.zh[:], zin[:], F.Copy, bias=-0.5), "zh", zi, 256)
        S_(lambda zin=zin: ACT(T.R[:, 4352:4608], zin[:], F.Copy), "Rz", zi, 256)
        V(lambda fin=fin: TT(xq, u32, fin[:], A.mult), "xq", "u32 " + fi, 16)
        V(lambda: TT(xq, xq, u2, A.add), "xq", "xq u2", 16)
        V(lambda: TS(T.CI[:, 16:32], xq, 5, 1023, A.arith_shift_right, A.bitwise_and), "ci", "xq", 16)
        V(lambda: TC(cu, T.CI[:, 16:32]), "cu", "ci", 16)
        V(lambda: TC(T.su[:], T.C[:, 0:1024].indirect(cu)), "su", "C cu", 256, 1.5)
        S_(lambda: ACT(T.sF[:], T.C[:, 0:1024].indirect(cu), F.Copy), "sF", "C cu", 256, 1.5)
        V(lambda: TT(ye, T.CI[:, 16:32], u32, A.mult), "ye", "ci u32", 16)
        V(lambda: TS(ye, ye, 32.0, None, A.add), "ye", "ye", 16)
        V(lambda: TS(T.CI[:, 32:48], ye, 5, 1023, A.arith_shift_right, A.bitwise_and), "ei", "ye", 16)
        V(lambda: TC(eu, T.CI[:, 32:48]), "eu", "ei", 16)
        V(lambda: TC(T.su2[:], T.C[:, 0:1024].indirect(eu)), "su2", "C eu", 256, 1.5)
        V(lambda: TS(T.CI[:, 0:16], ui, 15, None, A.bitwise_and), "mi", "ui", 16)
        V(lambda: TC(T.L3[:], T.CI[:]), "L3", "ci mi ei", 48)
        V(lambda: TC(cf, T.CI[:, 16:32]), "cf", "ci", 16)
        V(lambda: TS(nek, T.CI[:, 32:48], -1.0, None, A.mult), "nek", "ei", 16)
        V(lambda: TT(T.RM[:], T.CI[:], T.K3[:], A.subtract), "RM", "ci mi ei K3", 48)
        PM([(T.b0[:, 256:512], T.Ih[:], T.r16h[:], True, False)] +
           [(T.b0[:, 256 + j:512:16], T.Sp[:, j, :], T.L3[:, 0:16], False, j == 15) for j in R16], 30, "b0", "Ih r16h Sp L3")
        spread("b4", 0, "L3", 16, 48)
        V(lambda: TC(T.crow[:], T.b4[:, 0:256]), "crow", "b4", 256)
        S_(lambda: ACT(T.erF[:], T.b4[:, 256:512], F.Copy), "erF", "b4", 256)
        for r in range(2):
            V(lambda r=r: TS(T.s16[:, :, r, :], T.su[:, 128 * r:128 * r + 128], -2048.0, None, A.add), "s16", "su", 128, 0.5)
        V(lambda: v.transpose(T.t16[:], T.s16[:]), "t16", "s16", 256, 0.5)
        PM([(T.b0[:, 0:256], W1, T.ckb[:], True, False)], 256, "b0", "W1 ckb")
        PM([(T.b0[:, 128 * r:128 * r + 128], T.W4[:, 2 * r + h, :], T.t16[:, :, 16 * h:16 * h + 16], False, False)
            for r in range(2) for h in range(2)], 128, "b0", "W4 t16")

        def records(eng, su, buf, out, lo, hi, key, okey):
            n = hi - lo
            win = T.R[:, 0:4096].indirect(T[su][:, lo // 16:hi // 16])
            xo = T[out][:, lo // 256:hi // 256, :]
            if eng == "v":
                V(lambda: TT(T[buf][:, lo:hi], win, T.ze[:, lo:hi], A.subtract), key, "R " + su + " " + ZE, n, 1.5)
                S_(lambda: ACT(xo, T[buf][:, lo:hi], F.Abs), okey, key, n)
                return
            bk = "b%d" % (6 + lo // 512 % 2)
            S_(lambda: ACT(T[buf][:, lo:hi], win, F.Copy), key, "R " + su, n, 1.5)
            PM([(T[bk][:], Ib, T[buf][:, lo:hi], True, False), (T[bk][:], In, T.ze[:, lo:hi], False, True)], 512, bk, "Ib In " + key + " " + ZE)
            S_(lambda: ACT(xo, T[bk][:], F.Abs), okey, bk, n)

        for k, (b0, nb) in enumerate(CH):
            lo, hi = 256 * b0, 256 * (b0 + nb)
            xl = []
            for y in range(lo, hi, hi - lo if CM[k] == "v" else 512):
                xl.append("xa.%d" % y)
                records(CM[k], "su", "x2", "xa", y, hi if CM[k] == "v" else y + 512, "x2.%d" % y, xl[-1])
            xl = " ".join(xl)
            PM([(T.b0[:, 16 * b0:16 * (b0 + nb)], T.Sk[:, j, :], T.xa[:, b0:b0 + nb, 16 * j:16 * j + 16], False, k == len(CH) - 1 and j == 15)
                for j in R16], 16 * nb, "b0", "Sk " + xl)
            PM([(T.b1[:, 16 * b0:16 * (b0 + nb)], T.Sb[:, j, :], T.xa[:, b0:b0 + nb, j:256:16], j == 0, j == 15)
                for j in R16], 16 * nb, "b1", "Sb " + xl)
        for k in range(8):
            records(EM[k], "su2", "ve", "xe", 512 * k, 512 * k + 512, "ve.%d" % k, "xe.%d" % k)
            if k % 2:
                b0 = 2 * k - 2
                PM([(T.b2[:, 16 * b0:16 * b0 + 64], T.Sb[:, j, :], T.xe[:, b0:b0 + 4, j:256:16], j == 0, j == 15)
                    for j in R16], 64, "b2", "Sb xe.%d xe.%d" % (k - 1, k))
        if t == 0:
            V(lambda: TC(T.hc[:, 0:1], T.thf[:, 0:1]), "h", "thf", 1)
        else:
            V(lambda: TC(T.ai[:], T.b3[:, 128:129]), "ai", "b3", 1)
            V(lambda: TS(T.ai[:], T.ai[:], 31, None, A.bitwise_and), "ai", "ai", 1)
            V(lambda t=t: TT(T.hc[:, 0:1], T.ai[:], T.thf[:, t:t + 1], A.add), "h", "ai thf", 1)
        V(lambda: TS(T.hm[:], T.hA[:], T.hc[:, 0:1], None, A.mult), "hm", "h hA", 4)
        V(lambda: TT(T.hc[:, 1:5], T.hm[:], T.hB[:], A.add), "hs", "hm hB", 4)
        V(lambda: v.tensor_tensor_scan(T.sm[:], T.d0n[:], T.b0[:, 0:256], 0.0, A.add, A.min), "sm", "d0n b0", 256)
        V(lambda: TS(T.sa_[:], T.b1[:, 0:256], T.hc[:, 0:1], 4.0, A.min, A.mult), "sa_", "b1 h", 256)
        V(lambda: TS(T.sb_[:], T.b1[:, 0:256], T.hc[:, 0:1], 512.0, A.max, A.min), "sb_", "b1 h", 256)
        V(lambda: TS(T.sq_[:], T.b1[:, 0:256], 512.0, T.hc[:, 3:4], A.is_ge, A.mult), "sq_", "b1 hs", 256)
        for k, n in enumerate(("sa_", "sb_", "sq_")):
            PM([(T.b3[:, 16:32], T.Sh[:, j, :], T[n][:, j:256:16], k == 0 and j == 0, k == 2 and j == 15) for j in R16], 16, "b3", "Sh " + n)
        V(lambda: TS(ps, T.b3[:, 16:32], T.hc[:, 4:5], None, A.is_le), "ps", "b3 hs", 16)
        sml = T.sm[:, 15:256:16]
        V(lambda: TS(has, sml, T.hc[:, 1:2], None, A.is_lt), "has", "sm hs", 16)
        V(lambda: TC(kI, sml), "kI", "sm", 16)
        V(lambda: TS(ny, kI, 4095, None, A.bitwise_and), "ny", "kI", 16)
        V(lambda: TT(t3, ny, zt, A.subtract), "t3", "ny zt", 16)
        V(lambda: TT(t4, t3, has, A.mult), "t4", "t3 has", 16)
        V(lambda: TT(t5, t4, zt, A.add), "t5", "t4 zt", 16)
        V(lambda: TC(zo, t5), "zo", "t5", 16)
        V(lambda: TT(T.xs[:], T.R[:].indirect(zo), T.zh[:], A.add), "xs", "R Rz zh zo", 256, 1.5)
        V(lambda: TS(T.x4[:], T.xs[:], 16777216.0, 16777216.0, A.add, A.subtract), "x4", "xs", 256, 0.5)
        V(lambda zout=zout: TS(zout[:], T.x4[:], 0.5, None, A.mult), zo_, "x4", 256, 0.5)
        send("z", zo_, "zin%d" % (t + 1), t)
        V(lambda: TC(nyu, ny), "nyu", "ny", 16)
        V(lambda: TS(T.pg[:], T.PT[:, 0:4096].indirect(nyu), -2048.0, None, A.add), "pg", "PT nyu", 256, 1.5)
        pick(T.b4[:, 256:272], "pg", "b4")
        V(lambda: TS(w1, kI, 16, None, A.arith_shift_right), "w1", "kI", 16)
        V(lambda: TS(w5, w1, 5.0, 5376.0, A.mult, A.add), "w5", "w1", 16)
        V(lambda fin=fin: TT(w6, w5, fin[:], A.add), "w6", "w5 " + fi, 16)
        V(lambda fin=fin: TS(f0a, fin[:], 5.0, 10240.0, A.mult, A.add), "f0a", fi, 16)
        V(lambda: TT(f0, f0a, ui, A.add), "f0", "f0a ui", 16)
        V(lambda: TT(w6, w6, f0, A.subtract), "w6", "w6 f0", 16)
        V(lambda: TT(dif, T.b4[:, 256:272], w6, A.add), "dif", "b4 w6", 16)
        V(lambda: TT(ph, ps, has, A.mult), "ph", "ps has", 16)
        V(lambda: TT(pdh, ph, dif, A.mult), "pdh", "ph dif", 16)
        dedupe("EQ", "b5", "v", T.crow, "crow", "cf", "ps")
        V(lambda: TT(rr, WB, pdh, A.mult), "rr", "b5 pdh", 16)
        V(lambda: TT(fr, rr, f0, A.add), "fr", "rr f0", 16)
        V(lambda: TS(fr2, fr, 4095, None, A.bitwise_and), "fr2", "fr", 16)
        V(lambda fout=fout: TS(fout[:], fr2, -2048.0, None, A.add), fo, "fr2", 16)
        send("f", fo, "fin%d" % (t + 1), t)
        V(lambda: TT(T.acc[:, 0:16], WB, ps, A.mult), "acc", "b5 ps", 16)
        V(lambda: TT(T.acc[:, 16:32], WB, ps, A.mult), "acc2", "b5 ps", 16)
        if t < NV - 1:
            S_(lambda: ACT(T.accb[:], T.acc[:, 0:16], F.Copy, accum_out=af), "accb af", "acc", 16)
            PM([(T.b3[:, 128:129], one, af, True, True)], 256, "b3", "one af")
        S_(lambda: ACT(T.mM[:], T.b0[:, 0:256], F.Relu, bias=-64.0 * 16777216.0, scale=64.0), "mM", "b0", 256)
        V(lambda: TT(T.kr[:], T.b0[:, 0:256], T.mM[:], A.subtract), "kr", "b0 mM", 256)
        V(lambda: v.tensor_tensor_scan(T.sx[:], T.d0x[:], T.kr[:], 0.0, A.add, A.max), "sx", "d0x kr", 256)
        sxl = T.sx[:, 15:256:16]
        V(lambda: TC(fI, sxl), "fI", "sx", 16)
        V(lambda: TS(foe, sxl, T.hc[:, 2:3], None, A.is_ge), "foe", "sx hs", 16)
        V(lambda: TS(vs, fI, 4095, None, A.bitwise_and), "vs", "fI", 16)
        V(lambda: TS(vk, vs, -2048.0, None, A.add), "vk", "vs", 16)
        V(lambda: TS(T.v16[:], vs, -2048.0, None, A.add), "v16", "vs", 16)
        V(lambda: TT(vrm, vs, tr, A.subtract), "vrm", "vs tr", 16)
        spread("b4", 0, "v16", 0, 16)
        V(lambda: TC(T.vrow[:], T.b4[:, 0:256]), "vrow", "b4", 256)
        V(lambda: TT(flg, foe, T.acc[:, 0:16], A.mult), "flg", "foe acc", 16)
        dedupe("EQv", "b5", "v", T.vrow, "vrow", "vk", "flg")
        V(lambda: TT(unq, WB, flg, A.mult), "unq", "b5 flg", 16)
        V(lambda: TT(dl, unq, vrm, A.mult), "dl", "unq vrm", 16)
        V(lambda: TT(dl, dl, tr, A.add), "dl", "dl tr", 16)
        V(lambda: TC(dlu, dl), "dlu", "dl", 16)
        V(lambda: TC(T.R[:, 0:4352].indirect(dlu), T.s64[:]), "R", "dlu s64", 256, 3.5)
        V(lambda: TT(T.la[:], T.acc[:], T.RM[:, 0:32], A.mult), "la", "acc acc2 RM", 32)
        V(lambda: TT(T.la[:], T.la[:], T.T2c[:], A.add), "la", "la T2c", 32)
        V(lambda: TC(T.lau[:], T.la[:]), "lau", "la", 32)
        V(lambda zout=zout: TC(T.R[:, 0:4352].indirect(T.lau[:, 0:16]), zout[:]), "R", "lau " + zo_, 256, 3.5)
        PM([(T.b4[:, 256 + j:512:16], T.Sp[:, j, :], fout[:], True, True) for j in R16], 16, "b4", "Sp " + fo)
        S_(lambda: ACT(T.phr[:], T.b4[:, 256:512], F.Copy, bias=2048.0), "phr", "b4", 256)
        V(lambda: TC(T.PT[:].indirect(T.lau[:, 0:16]), T.phr[:]), "PT", "lau phr", 256, 3.5)
        S_(lambda: ACT(T.sg[:], T.b1[:, 0:256], F.Sign, bias=-511.5), "sg", "b1", 256)
        PM([(T.b1[:, 256:512], Y1, T.sg[:], True, True)], 256, "b1", "Y1 sg")
        S_(lambda: ACT(T.b1[:, 256:512], T.b1[:, 256:512], F.Relu, bias=bn), "b1", "bn", 256)
        V(lambda: TT(T.nd[:], T.b0[:, 256:512], T.sF[:], A.subtract), "nd", "b0 sF", 256)
        V(lambda: TT(T.nd[:], T.nd[:], T.b1[:, 256:512], A.mult), "nd", "nd b1", 256)
        V(lambda: TT(T.C[:].indirect(T.lau[:, 16:32]), T.nd[:], T.sF[:], A.add), "C", "lau nd sF", 256, 3.5)
        S_(lambda: ACT(T.sup[:], T.b2[:, 0:256], F.Relu, bias=T.hc[:, 0:1], scale=-1.0), "sup", "b2 h", 256)
        S_(lambda: ACT(T.sg2[:], T.b2[:, 0:256], F.Sign, bias=-511.5), "sg2", "b2", 256)
        PM([(T.b2[:, 256:512], Y2, T.sg2[:], True, True)], 256, "b2", "Y2 sg2")
        S_(lambda: ACT(T.b2[:, 256:512], T.b2[:, 256:512], F.Relu, bias=bx), "b2", "bx", 256)
        PM([(T.b7[:, 0:16], T.Sb[:, j, :], T.sup[:, j:256:16], j == 0, j == 15) for j in R16], 16, "b7", "Sb sup")
        V(lambda: TS(cn0, T.b7[:, 0:16], 0.0, None, A.is_equal), "cn0", "b7", 16)
        V(lambda: TT(cnd, cn0, T.acc[:, 0:16], A.mult), "cnd", "cn0 acc", 16)
        dedupe("EQe", "b6", "a", T.erF, "erF", "nek", "cnd")
        V(lambda: TT(w2, T.b6[:, 256:272], cnd, A.mult), "w2", "b6 cnd", 16)
        V(lambda: TT(l2, w2, T.RM[:, 32:48], A.mult), "l2", "w2 RM", 16)
        V(lambda: TT(l2, l2, tc, A.add), "l2", "l2 tc", 16)
        V(lambda: TC(l2u, l2), "l2u", "l2", 16)
        S_(lambda: ACT(T.sF2[:], T.C[:, 0:1024].indirect(eu), F.Copy), "sF2", "C eu", 256, 1.5)
        V(lambda: TT(T.nd2[:], T.b0[:, 256:512], T.sF2[:], A.subtract), "nd2", "b0 sF2", 256)
        V(lambda: TT(T.nd2[:], T.nd2[:], T.b2[:, 256:512], A.mult), "nd2", "nd2 b2", 256)
        V(lambda: TT(T.C[:].indirect(l2u), T.nd2[:], T.sF2[:], A.add), "C", "l2u nd2 sF2", 256, 3.5)
    D("yrec", T.yrec[:], T.R[:, 0:4096], "", "R", 6.0)
    D("ycel", T.ycel[:], T.C[:, 0:1024], "", "C", 4.0, "a")
    D("ypo", T.ypo[:], T.PT[0:128:16, 0:4096], "", "PT", 3.0)
    zl, fl = "zin%d" % NV, "fin%d" % NV
    D("ypat", T.ypat[:], T[zl][:], "", zl, 2.0)
    spread("b4", 0, fl, 0, 16)
    V(lambda: TS(T.phr[:], T.b4[:, 0:256], 2048.0, None, A.add), "phr", "b4", 256)
    D("yphi", T.yphi[:], T.phr[0:128:16, :], "", "phr", 2.0)
    return ops


def schedule(ops):
    n = len(ops)
    succ = [[] for _ in ops]
    need = [0] * n
    for o in ops:
        deps = o["wait"] | o["ord"] | ({o["net"]} if o["net"] is not None else set())
        need[o["i"]] = len(deps)
        for x in sorted(deps):
            succ[x].append(o["i"])
    pri = [0.0] * n
    for i in range(n - 1, -1, -1):
        pri[i] = ops[i]["d"] + max([pri[k] + 0.1 for k in succ[i]] or [0.0])
    free = {q: 0.0 for q in "vapgs"}
    ready = {q: [] for q in "vapgsn"}
    at = [0.0] * n
    for i in range(n):
        if need[i] == 0:
            ready[ops[i]["q"]].append(i)
    order = []
    while len(order) < n:
        st, q = min((max(free.get(q, 0.0), min(at[i] for i in L)), q) for q, L in ready.items() if L)
        i = max((i for i in ready[q] if at[i] <= st + 1e-9), key=lambda i: pri[i])
        ready[q].remove(i)
        o = ops[i]
        if q != "n":
            free[q] = st + (o["d"] if o["sem"] is None else 0.1)
        end = st + o["d"]
        order.append(i)
        for k in succ[i]:
            need[k] -= 1
            same = ops[k]["q"] == q
            at[k] = max(at[k], st if same and i not in ops[k]["wait"] else end + (0.03 if same else 0.1))
            if need[k] == 0:
                ready[ops[k]["q"]].append(k)
    return order


def rank_program(g, core, T, topo):
    rank = T.rank_of(core)
    if rank is None:
        return
    nxt = T.cores[(rank + 1) % len(T.cores)]
    ops = program(T, g, core, nxt, topo)
    eng = {"v": g.vector, "a": g.scalar, "p": g.tensor, "g": g, "s": g.sync}
    cnt = {q: 0 for q in "vapg"}
    seen = {q: {} for q in "vapgs"}
    clock, ev, final = {}, {}, {}
    for i in schedule(ops):
        o = ops[i]
        q = o["q"]
        if q == "n":
            ev[i] = (o["sem"], o["val"])
            clock[i] = {o["sem"]: o["val"]}
            final[o["sem"]] = o["val"]
            continue
        for x in sorted(o["wait"], key=lambda x: (-ev[x][1], x)):
            sm, val = ev[x]
            if seen[q].get(sm, 0) < val:
                eng[q].wait_ge(T.sem[sm], val)
                for k, y in clock[x].items():
                    if seen[q].get(k, 0) < y:
                        seen[q][k] = y
        for f in o["f"]:
            ins = f()
            if o["sem"] is None:
                ins.then_inc(T.sem["q" + q], 1)
                cnt[q] += 1
            elif o["sem"][0] == "d":
                ins.then_inc(T.sem[o["sem"]], 16)
        ev[i] = (o["sem"], o["val"]) if o["sem"] else ("q" + q, cnt[q])
        clock[i] = dict(seen[q])
        clock[i][ev[i][0]] = ev[i][1]
        final[ev[i][0]] = ev[i][1]
    for sm, val in final.items():
        g.wait_ge(T.sem[sm], val)
